import numpy as np
import ml_dtypes


def mxq(x, axis, fmt="e4m3"):
    dtype, down = {"e4m3": (ml_dtypes.float8_e4m3fn, 7), "e5m2": (ml_dtypes.float8_e5m2, 14)}[fmt]
    v = np.moveaxis(np.asarray(x, np.float32).astype(ml_dtypes.bfloat16).astype(np.float64), axis, -1)
    blocks = v.reshape(v.shape[:-1] + (-1, 32))
    amax = np.abs(blocks).max(-1, keepdims=True)
    byte = np.maximum(np.where(amax > 0, np.frexp(amax)[1] - 1 + 127, 0) - down, 1)
    scale = np.exp2(byte - 127.0)
    codes = (blocks / scale).astype(np.float32).astype(dtype).astype(np.float64)
    return np.moveaxis((codes * scale).reshape(v.shape), -1, axis)


WIDE = False


def mx_kscale(k):
    if not WIDE:
        return np.ones(k)
    levels = np.array([10, -10, 5, -5, 0])
    if k % 512:
        return np.exp2(np.random.permutation(np.resize(levels, k // 32))).repeat(32)
    a = np.empty((k // 512, 16))
    for p in range(k // 512):
        a[p, :8] = np.random.permutation(np.resize(levels, 8))
        for g in range(8):
            far = levels[np.abs(levels - a[p, g]) >= 10]
            a[p, g + 8] = far[np.random.randint(len(far))]
    return np.exp2(a.ravel()).repeat(32)


def f64(x):
    return np.asarray(x).astype(np.float64)


def striped(idx):
    return np.tile(np.asarray(idx).reshape(-1, 16).T, (8, 1)).astype(np.uint16)


def unstriped(offs):
    return offs[:16].T.reshape(-1).astype(np.int64)


def bf(x):
    return np.asarray(x, np.float32).astype(ml_dtypes.bfloat16)


def planes(Y):
    r, m = Y.shape
    b = f64(bf(Y)).reshape(r // 32, 32, m)
    amax = np.abs(b).max(1)
    byte = np.clip(np.where(amax > 0, np.frexp(amax)[1] - 1 + 127 - 7, 1), 1, 254)
    codes = (b * np.exp2(127.0 - byte)[:, None, :]).reshape(r, m).astype(np.float32).astype(ml_dtypes.float8_e4m3fn).view(np.uint8)
    words = codes.reshape(r // 512, 128, 4, m).transpose(0, 1, 3, 2)
    return np.ascontiguousarray(words), np.ascontiguousarray(byte.astype(np.uint8).reshape(r // 512, 16, m))


K, T, I, G, U, D = 512, 2048, 1024, 256, 1024, 512


def setup_inputs():
    n = np.random.standard_normal
    idx = np.random.permutation(T)[:I]
    idx2 = np.random.permutation(U)[:G]
    fk = mx_kscale(K)
    return {
        "hid": (n((K, T)) * 2.0 / fk[:, None]).astype(np.float32),
        "wp": (n((K, D)) * 1 / np.sqrt(K) * fk[:, None]).astype(np.float32),
        "bias": (np.random.uniform(-0.5, 0.5, (D, 1))).astype(np.float32),
        "old": (n((D, U))).astype(np.float32),
        "fade": (np.random.uniform(0.5, 1.0, (1, U))).astype(np.float32),
        "offs": striped(idx),
        "offs2": striped(idx2),
    }


def reference(hid, wp, bias, old, fade, offs, offs2):
    idx = unstriped(offs)
    idx2 = unstriped(offs2)
    hs = f64(hid)[:, idx].reshape(K, G, I // G).mean(axis=2)
    wpq = mxq(f64(wp), 0, "e4m3")
    hsq = mxq(hs, 0, "e4m3")
    z = wpq.T @ hsq
    b = np.tanh(z + f64(bias))
    bf = np.zeros((D, U))
    bf[:, idx2] = b
    y = f64(old) * f64(fade) + bf
    words, scales = planes(y)
    return y, words, scales

@@ -1,0 +1,214 @@
+from contextlib import ExitStack
+
+import concourse.mybir as mybir
+from concourse.masks import make_identity
+
+K, T, I, G, U, D = 512, 2048, 1024, 256, 1024, 512
+FLOPS = 2 * K * D * G
+
+F32 = mybir.dt.float32
+BF16 = mybir.dt.bfloat16
+I32 = mybir.dt.int32
+U32 = mybir.dt.uint32
+U16 = mybir.dt.uint16
+U8 = mybir.dt.uint8
+FP8X4 = mybir.dt.float8_e4m3fn_x4
+ACT = mybir.ActivationFunctionType
+ALU = mybir.AluOpType
+AX = mybir.AxisListType
+
+P = 128
+PACK = 4
+PAGE = I // G
+UB = U // P
+
+
+def tile_attend_summaryrefresh_pl_kernel(tc, hid, wp, bias, old, fade, offs, offs2, out_0, out_1, out_2):
+    nc = tc.nc
+    hid_planes = hid.rearrange("(p t) n -> p t n", t=PACK)
+    old_planes = old.rearrange("(p t) u -> p t u", t=PACK)
+    out_planes = out_0.rearrange("(p t) u -> p t u", t=PACK)
+    wp_rows = wp.rearrange("(p j) c -> p j c", j=PACK)
+
+    with ExitStack() as ctx:
+        keep = ctx.enter_context(tc.tile_pool(name="keep", bufs=1))
+        ring = ctx.enter_context(tc.psum_pool(name="ring", bufs=2))
+        zpool = ctx.enter_context(tc.psum_pool(name="zpool", bufs=2))
+        wide = ctx.enter_context(tc.psum_pool(name="wide", bufs=4))
+
+        slots = keep.tile([P, I // 16], U16, name="slots")
+        pages = keep.tile([P, G // 16], U16, name="pages")
+        nc.sync.dma_start(slots[:], offs)
+        pool = []
+        for t in range(PACK):
+            plane = keep.tile([P, T], F32, name=f"pool{t}")
+            nc.sync.dma_start(plane[:], hid_planes[:, t, :])
+            pool.append(plane)
+        w_raw = []
+        for h in range(2):
+            half = keep.tile([P, PACK, D // 2], F32, name=f"w_raw{h}")
+            nc.sync.dma_start(half[:], wp_rows[:, :, h * (D // 2):(h + 1) * (D // 2)])
+            w_raw.append(half)
+        nc.sync.dma_start(pages[:], offs2)
+        bias4 = keep.tile([P, PACK], F32, name="bias4")
+        nc.sync.dma_start(bias4[:], bias.rearrange("(p t) o -> p (t o)", t=PACK))
+        olds = {}
+        for t in (0, 1, 3, 2):
+            plane = keep.tile([P, U], F32, name=f"old{t}")
+            nc.sync.dma_start(plane[:], old_planes[:, t, :])
+            olds[t] = plane
+
+        warm = keep.tile([P, 2], F32, name="warm")
+        nc.vector.memset(warm[:, 0:1], 0.0)
+        nc.scalar.activation(warm[:, 1:2], warm[:, 0:1], ACT.Tanh)
+        fade_rows = keep.tile([P, P], F32, name="fade_rows")
+        nc.gpsimd.memset(fade_rows[:], 0.0)
+        nc.scalar.dma_start(fade_rows[0:UB, :], fade.rearrange("o (b q) -> (o b) q", b=UB))
+        ident = keep.tile([P, P], F32, name="ident")
+        make_identity(nc, ident[:])
+        placed = []
+        for t in range(PACK):
+            window = keep.tile([P, U], F32, name=f"placed{t}")
+            nc.vector.memset(window[:], 0.0)
+            placed.append(window)
+
+        fade_turned = wide.tile([P, 512], F32, name="fade_turned", tag="wide")
+        nc.tensor.transpose(fade_turned[:, 0:P], fade_rows[:], ident[:])
+        fade_cols = keep.tile([P, UB], F32, name="fade_cols")
+        nc.scalar.copy(fade_cols[:], fade_turned[:, 0:UB])
+        fade_all = keep.tile([P, U], F32, name="fade_all")
+        for h in range(2):
+            spread = wide.tile([P, 512], F32, name="spread", tag="wide")
+            for q in range(4):
+                b = 4 * h + q
+                nc.tensor.transpose(spread[:, q * P:(q + 1) * P], fade_cols[:, b:b + 1].to_broadcast([P, P]), ident[:])
+            nc.scalar.copy(fade_all[:, h * 512:(h + 1) * 512], spread[:])
+
+        hs_bf = keep.tile([P, G, PACK], BF16, name="hs_bf", align_bytes=64)
+        sums_turned = ring.tile([P, 2, 2, P], F32, name="sums_turned", tag="ring")
+        for t in range(2):
+            picked = keep.tile([P, I], F32, name=f"picked{t}")
+            nc.vector.tensor_copy(picked[:], pool[t][:].indirect(slots[:]))
+            for gb in range(2):
+                for j in range(PAGE):
+                    nc.tensor.matmul(
+                        sums_turned[:, t, gb, :],
+                        lhsT=picked[:, gb * 512 + j:(gb + 1) * 512:PAGE],
+                        rhs=ident[:],
+                        start=(j == 0),
+                        stop=(j == PAGE - 1),
+                        is_transpose=True,
+                    )
+        pairs_turned = keep.tile([P, 2, P, 2], BF16, name="pairs_turned")
+        nc.scalar.activation(pairs_turned[:], sums_turned[:].rearrange("g e b p -> g b p e"), ACT.Copy, scale=1.0 / PAGE)
+        pairs = ring.tile([P, 512], F32, name="pairs", tag="ring")
+        for gb in range(2):
+            nc.tensor.transpose(
+                pairs[:, gb * P:(gb + 1) * P],
+                pairs_turned[:, gb].rearrange("g p e -> g (p e)").bitcast(F32),
+                ident[:],
+            )
+        hs_words = hs_bf[:].rearrange("p g t -> p (g t)").bitcast(F32)
+        nc.scalar.copy(hs_words[:, 0:2 * G:2], pairs[:, 0:G])
+
+        sums = keep.tile([P, 2, G], F32, name="sums")
+        picked2 = keep.tile([P, G, PAGE], F32, name="picked2")
+        nc.vector.tensor_copy(picked2[:].rearrange("p g j -> p (g j)"), pool[2][:].indirect(slots[:]))
+        halves = keep.tile([P, G, 2], F32, name="halves")
+        nc.gpsimd.tensor_tensor(halves[:], picked2[:, :, 0:2], picked2[:, :, 2:4], ALU.add)
+        nc.gpsimd.tensor_tensor(sums[:, 0, :], halves[:, :, 0], halves[:, :, 1], ALU.add)
+        picked3 = keep.tile([P, G, PAGE], F32, name="picked3")
+        nc.vector.tensor_copy(picked3[:].rearrange("p g j -> p (g j)"), pool[3][:].indirect(slots[:]))
+        nc.vector.tensor_reduce(sums[:, 1, :], picked3[:], AX.X, ALU.add)
+        nc.vector.tensor_scalar(hs_bf[:, :, 2:4], sums[:].rearrange("p e g -> p g e"), 1.0 / PAGE, None, ALU.mult)
+
+        w_bf = keep.tile([P, PACK, P, PACK], BF16, name="w_bf", align_bytes=64)
+        for h in range(2):
+            nc.scalar.copy(
+                w_bf[:, :, h * 64:(h + 1) * 64, :].rearrange("p t m j -> p m t j"),
+                w_raw[h][:].rearrange("p j (m t) -> p m t j", t=PACK),
+            )
+        hs_codes = keep.tile([P, G], U32, name="hs_codes", align_bytes=64)
+        hs_scales = keep.tile([P, G], U8, name="hs_scales", align_bytes=64)
+        nc.vector.quantize_mx(hs_codes[:].bitcast(FP8X4), hs_scales[:], hs_bf[:].rearrange("p g t -> p (g t)"))
+        fresh = []
+        for t in range(PACK):
+            w_codes = keep.tile([P, P], U32, name=f"w_codes{t}", align_bytes=64)
+            w_scales = keep.tile([P, P], U8, name=f"w_scales{t}", align_bytes=64)
+            nc.vector.quantize_mx(w_codes[:].bitcast(FP8X4), w_scales[:], w_bf[:, t].rearrange("p m j -> p (m j)"))
+            z = zpool.tile([P, G], F32, name="z", tag="z")
+            nc.tensor.matmul_mx(
+                z[:], lhsT=w_codes[:].bitcast(FP8X4), lhsT_scale=w_scales[:],
+                rhs=hs_codes[:].bitcast(FP8X4), rhs_scale=hs_scales[:], start=True, stop=True,
+            )
+            b = keep.tile([P, G], F32, name=f"fresh{t}")
+            nc.scalar.activation(b[:], z[:], ACT.Tanh, bias=bias4[:, t:t + 1])
+            fresh.append(b)
+
+        faded = {}
+        for t in (0, 2):
+            product = keep.tile([P, U], F32, name=f"faded{t}")
+            faded[t] = product
+        nc.gpsimd.tensor_tensor(faded[0][:], olds[0][:], fade_all[:], ALU.mult)
+        for t in (1, 3):
+            turned_sb = keep.tile([P, UB, P], F32, name=f"turned_sb{t}")
+            for h in range(2):
+                turned = ring.tile([P, 512], F32, name="turned", tag="ring")
+                for q in range(4):
+                    b = 4 * h + q
+                    nc.tensor.transpose(turned[:, q * P:(q + 1) * P], olds[t][:, b * P:(b + 1) * P], ident[:])
+                for q in range(4):
+                    b = 4 * h + q
+                    nc.scalar.activation(
+                        turned_sb[:, b, :], turned[:, q * P:(q + 1) * P], ACT.Copy, scale=fade_cols[:, b:b + 1]
+                    )
+            banks = []
+            for h in range(2):
+                back = wide.tile([P, 512], F32, name="back", tag="wide")
+                for q in range(4):
+                    nc.tensor.transpose(back[:, q * P:(q + 1) * P], turned_sb[:, 4 * h + q, :], ident[:])
+                banks.append(back)
+            faded[t] = banks
+
+        ys = [keep.tile([P, 2, U], F32, name=f"y{e}") for e in range(2)]
+        y_bf = keep.tile([P, U, PACK], BF16, name="y_bf", align_bytes=64)
+
+        def scatter(t):
+            nc.vector.tensor_copy(placed[t][:].indirect(pages[:]), fresh[t][:])
+
+        def store(t):
+            nc.sync.dma_start(out_planes[:, t, :], ys[t // 2][:, t % 2, :])
+
+        scatter(0)
+        nc.gpsimd.tensor_tensor(ys[0][:, 0, :], faded[0][:], placed[0][:], ALU.add)
+        store(0)
+        scatter(1)
+        nc.gpsimd.tensor_tensor(faded[2][:], olds[2][:], fade_all[:], ALU.mult)
+        scatter(2)
+        for h in range(2):
+            cols = slice(h * 512, (h + 1) * 512)
+            nc.vector.tensor_tensor(ys[0][:, 1, cols], faded[1][h][:], placed[1][:, cols], ALU.add)
+        store(1)
+        nc.gpsimd.tensor_tensor(ys[1][:, 0, :], faded[2][:], placed[2][:], ALU.add)
+        store(2)
+        nc.scalar.copy(y_bf[:, :, 0:2], ys[0][:].rearrange("p e u -> p u e"))
+        scatter(3)
+        y_codes = keep.tile([P, U], U32, name="y_codes", align_bytes=64)
+        y_scales = keep.tile([P, U], U8, name="y_scales", align_bytes=64)
+        words_out = out_1[0].rearrange("l c r -> l (c r)").bitcast(I32)
+        for h in range(2):
+            cols = slice(h * 512, (h + 1) * 512)
+            nc.vector.tensor_tensor(ys[1][:, 1, cols], faded[3][h][:], placed[3][:, cols], ALU.add)
+        store(3)
+        for h in range(2):
+            cols = slice(h * 512, (h + 1) * 512)
+            nc.vector.tensor_copy(y_bf[:, cols, 2:4], ys[1][:, :, cols].rearrange("p e u -> p u e"))
+        for h in range(2):
+            cols = slice(h * 512, (h + 1) * 512)
+            nc.vector.quantize_mx(
+                y_codes[:, cols].bitcast(FP8X4), y_scales[:, cols], y_bf[:, cols, :].rearrange("p u t -> p (u t)")
+            )
+            nc.sync.dma_start(words_out[:, cols], y_codes[:, cols].bitcast(I32))
+        for q in range(4):
+            engine = nc.sync if q % 2 == 0 else nc.scalar
+            engine.dma_start(out_2[0, 4 * q:4 * q + 4, :].bitcast(I32), y_scales[32 * q:32 * q + 4, :].bitcast(I32))

@@ -32,60 +32,60 @@ def tile_attend_summaryrefresh_pl_kernel(tc, hid, wp, bias, old, fade, offs, off
 
     with ExitStack() as ctx:
         keep = ctx.enter_context(tc.tile_pool(name="keep", bufs=1))
-        ring = ctx.enter_context(tc.psum_pool(name="ring", bufs=2))
-        zpool = ctx.enter_context(tc.psum_pool(name="zpool", bufs=2))
-        wide = ctx.enter_context(tc.psum_pool(name="wide", bufs=4))
+        psum = ctx.enter_context(tc.psum_pool(name="psum", bufs=1))
+
+        def bank(index, shape, name):
+            return psum.tile(shape, F32, name=name, tag=f"bank{index}")
 
         slots = keep.tile([P, I // 16], U16, name="slots")
         pages = keep.tile([P, G // 16], U16, name="pages")
-        nc.sync.dma_start(slots[:], offs)
+        fade_rows = keep.tile([P, P], F32, name="fade_rows")
+        nc.gpsimd.memset(fade_rows[:], 0.0)
         pool = []
         for t in range(PACK):
             plane = keep.tile([P, T], F32, name=f"pool{t}")
             nc.sync.dma_start(plane[:], hid_planes[:, t, :])
             pool.append(plane)
-        w_raw = []
-        for h in range(2):
-            half = keep.tile([P, PACK, D // 2], F32, name=f"w_raw{h}")
-            nc.sync.dma_start(half[:], wp_rows[:, :, h * (D // 2):(h + 1) * (D // 2)])
-            w_raw.append(half)
+            if t == 0:
+                nc.sync.dma_start(slots[:], offs)
+                nc.sync.dma_start(fade_rows[0:UB, :], fade.rearrange("o (b q) -> (o b) q", b=UB))
+        w_raw = keep.tile([P, PACK, D], F32, name="w_raw")
+        nc.sync.dma_start(w_raw[:], wp_rows)
         nc.sync.dma_start(pages[:], offs2)
         bias4 = keep.tile([P, PACK], F32, name="bias4")
         nc.sync.dma_start(bias4[:], bias.rearrange("(p t) o -> p (t o)", t=PACK))
-        olds = {}
-        for t in (0, 1, 3, 2):
-            plane = keep.tile([P, U], F32, name=f"old{t}")
-            nc.sync.dma_start(plane[:], old_planes[:, t, :])
-            olds[t] = plane
+        halves_u = [slice(h * 512, (h + 1) * 512) for h in range(2)]
+        olds = []
+        for h, cols in enumerate(halves_u):
+            half = keep.tile([P, PACK, 512], F32, name=f"old{h}")
+            nc.sync.dma_start(half[:], old_planes[:, :, cols])
+            olds.append(half)
 
         warm = keep.tile([P, 2], F32, name="warm")
         nc.vector.memset(warm[:, 0:1], 0.0)
         nc.scalar.activation(warm[:, 1:2], warm[:, 0:1], ACT.Tanh)
-        fade_rows = keep.tile([P, P], F32, name="fade_rows")
-        nc.gpsimd.memset(fade_rows[:], 0.0)
-        nc.scalar.dma_start(fade_rows[0:UB, :], fade.rearrange("o (b q) -> (o b) q", b=UB))
         ident = keep.tile([P, P], F32, name="ident")
         make_identity(nc, ident[:])
         placed = []
         for t in range(PACK):
             window = keep.tile([P, U], F32, name=f"placed{t}")
-            nc.vector.memset(window[:], 0.0)
+            (nc.vector if t < 2 else nc.gpsimd).memset(window[:], 0.0)
             placed.append(window)
 
-        fade_turned = wide.tile([P, 512], F32, name="fade_turned", tag="wide")
-        nc.tensor.transpose(fade_turned[:, 0:P], fade_rows[:], ident[:])
-        fade_cols = keep.tile([P, UB], F32, name="fade_cols")
-        nc.scalar.copy(fade_cols[:], fade_turned[:, 0:UB])
+        fade_down = bank(2, [P, P], "fade_down")
+        nc.tensor.transpose(fade_down[:], fade_rows[:], ident[:])
+        fade_cols = keep.tile([P, UB], F32, name="fade_cols", tag="fade_cols", align_bytes=64)
+        nc.scalar.copy(fade_cols[:], fade_down[:, 0:UB])
         fade_all = keep.tile([P, U], F32, name="fade_all")
-        for h in range(2):
-            spread = wide.tile([P, 512], F32, name="spread", tag="wide")
+        for h, cols in enumerate(halves_u):
+            spread = bank(3 + h, [P, 512], "spread")
             for q in range(4):
                 b = 4 * h + q
                 nc.tensor.transpose(spread[:, q * P:(q + 1) * P], fade_cols[:, b:b + 1].to_broadcast([P, P]), ident[:])
-            nc.scalar.copy(fade_all[:, h * 512:(h + 1) * 512], spread[:])
+            nc.scalar.copy(fade_all[:, cols], spread[:])
 
         hs_bf = keep.tile([P, G, PACK], BF16, name="hs_bf", align_bytes=64)
-        sums_turned = ring.tile([P, 2, 2, P], F32, name="sums_turned", tag="ring")
+        sums_turned = bank(0, [P, 2, 2, P], "sums_turned")
         for t in range(2):
             picked = keep.tile([P, I], F32, name=f"picked{t}")
             nc.vector.tensor_copy(picked[:], pool[t][:].indirect(slots[:]))
@@ -101,7 +101,7 @@ def tile_attend_summaryrefresh_pl_kernel(tc, hid, wp, bias, old, fade, offs, off
                     )
         pairs_turned = keep.tile([P, 2, P, 2], BF16, name="pairs_turned")
         nc.scalar.activation(pairs_turned[:], sums_turned[:].rearrange("g e b p -> g b p e"), ACT.Copy, scale=1.0 / PAGE)
-        pairs = ring.tile([P, 512], F32, name="pairs", tag="ring")
+        pairs = bank(1, [P, 512], "pairs")
         for gb in range(2):
             nc.tensor.transpose(
                 pairs[:, gb * P:(gb + 1) * P],
@@ -112,99 +112,96 @@ def tile_attend_summaryrefresh_pl_kernel(tc, hid, wp, bias, old, fade, offs, off
         nc.scalar.copy(hs_words[:, 0:2 * G:2], pairs[:, 0:G])
 
         sums = keep.tile([P, 2, G], F32, name="sums")
-        picked2 = keep.tile([P, G, PAGE], F32, name="picked2")
-        nc.vector.tensor_copy(picked2[:].rearrange("p g j -> p (g j)"), pool[2][:].indirect(slots[:]))
-        halves = keep.tile([P, G, 2], F32, name="halves")
-        nc.gpsimd.tensor_tensor(halves[:], picked2[:, :, 0:2], picked2[:, :, 2:4], ALU.add)
-        nc.gpsimd.tensor_tensor(sums[:, 0, :], halves[:, :, 0], halves[:, :, 1], ALU.add)
-        picked3 = keep.tile([P, G, PAGE], F32, name="picked3")
-        nc.vector.tensor_copy(picked3[:].rearrange("p g j -> p (g j)"), pool[3][:].indirect(slots[:]))
-        nc.vector.tensor_reduce(sums[:, 1, :], picked3[:], AX.X, ALU.add)
+
+        def gather(t, first, count):
+            part = keep.tile([P, count, PAGE], F32, name=f"picked{t}_{first}")
+            columns = slice(first * PAGE // 16, (first + count) * PAGE // 16)
+            nc.vector.tensor_copy(part[:].rearrange("p g j -> p (g j)"), pool[t][:].indirect(slots[:, columns]))
+            return part
+
+        def sum_in_two_steps(part, into):
+            halves = keep.tile([P, part.shape[1], 2], F32, name="halves", tag="halves", bufs=2)
+            nc.gpsimd.tensor_tensor(halves[:], part[:, :, 0:2], part[:, :, 2:4], ALU.add)
+            nc.gpsimd.tensor_tensor(into, halves[:, :, 0], halves[:, :, 1], ALU.add)
+
+        sum_in_two_steps(gather(2, 0, G), sums[:, 0, :])
+        sum_in_two_steps(gather(3, 0, G // 2), sums[:, 1, 0:G // 2])
+        nc.vector.tensor_reduce(sums[:, 1, G // 2:G], gather(3, G // 2, G // 2)[:], AX.X, ALU.add)
         nc.vector.tensor_scalar(hs_bf[:, :, 2:4], sums[:].rearrange("p e g -> p g e"), 1.0 / PAGE, None, ALU.mult)
 
-        w_bf = keep.tile([P, PACK, P, PACK], BF16, name="w_bf", align_bytes=64)
-        for h in range(2):
+        w_bf = keep.tile([P, PACK, P, PACK], BF16, name="w_bf", tag="w_bf", align_bytes=64)
+        for ts in (slice(0, 2), slice(2, PACK)):
             nc.scalar.copy(
-                w_bf[:, :, h * 64:(h + 1) * 64, :].rearrange("p t m j -> p m t j"),
-                w_raw[h][:].rearrange("p j (m t) -> p m t j", t=PACK),
+                w_bf[:, ts].rearrange("p t m j -> p m j t"),
+                w_raw[:].rearrange("p j (m t) -> p m j t", t=PACK)[:, :, :, ts],
             )
+
         hs_codes = keep.tile([P, G], U32, name="hs_codes", align_bytes=64)
         hs_scales = keep.tile([P, G], U8, name="hs_scales", align_bytes=64)
         nc.vector.quantize_mx(hs_codes[:].bitcast(FP8X4), hs_scales[:], hs_bf[:].rearrange("p g t -> p (g t)"))
-        fresh = []
+        zs = []
         for t in range(PACK):
             w_codes = keep.tile([P, P], U32, name=f"w_codes{t}", align_bytes=64)
             w_scales = keep.tile([P, P], U8, name=f"w_scales{t}", align_bytes=64)
             nc.vector.quantize_mx(w_codes[:].bitcast(FP8X4), w_scales[:], w_bf[:, t].rearrange("p m j -> p (m j)"))
-            z = zpool.tile([P, G], F32, name="z", tag="z")
+            z = bank(4 + t, [P, G], f"z{t}")
             nc.tensor.matmul_mx(
                 z[:], lhsT=w_codes[:].bitcast(FP8X4), lhsT_scale=w_scales[:],
                 rhs=hs_codes[:].bitcast(FP8X4), rhs_scale=hs_scales[:], start=True, stop=True,
             )
+            zs.append(z)
+
+        for t in range(PACK):
             b = keep.tile([P, G], F32, name=f"fresh{t}")
-            nc.scalar.activation(b[:], z[:], ACT.Tanh, bias=bias4[:, t:t + 1])
-            fresh.append(b)
+            nc.scalar.activation(b[:], zs[t][:], ACT.Tanh, bias=bias4[:, t:t + 1])
+            nc.vector.tensor_copy(placed[t][:].indirect(pages[:]), b[:])
 
-        faded = {}
-        for t in (0, 2):
-            product = keep.tile([P, U], F32, name=f"faded{t}")
-            faded[t] = product
-        nc.gpsimd.tensor_tensor(faded[0][:], olds[0][:], fade_all[:], ALU.mult)
-        for t in (1, 3):
-            turned_sb = keep.tile([P, UB, P], F32, name=f"turned_sb{t}")
-            for h in range(2):
-                turned = ring.tile([P, 512], F32, name="turned", tag="ring")
-                for q in range(4):
-                    b = 4 * h + q
-                    nc.tensor.transpose(turned[:, q * P:(q + 1) * P], olds[t][:, b * P:(b + 1) * P], ident[:])
-                for q in range(4):
-                    b = 4 * h + q
-                    nc.scalar.activation(
-                        turned_sb[:, b, :], turned[:, q * P:(q + 1) * P], ACT.Copy, scale=fade_cols[:, b:b + 1]
-                    )
-            banks = []
-            for h in range(2):
-                back = wide.tile([P, 512], F32, name="back", tag="wide")
-                for q in range(4):
-                    nc.tensor.transpose(back[:, q * P:(q + 1) * P], turned_sb[:, 4 * h + q, :], ident[:])
-                banks.append(back)
-            faded[t] = banks
-
-        ys = [keep.tile([P, 2, U], F32, name=f"y{e}") for e in range(2)]
-        y_bf = keep.tile([P, U, PACK], BF16, name="y_bf", align_bytes=64)
-
-        def scatter(t):
-            nc.vector.tensor_copy(placed[t][:].indirect(pages[:]), fresh[t][:])
-
-        def store(t):
-            nc.sync.dma_start(out_planes[:, t, :], ys[t // 2][:, t % 2, :])
-
-        scatter(0)
-        nc.gpsimd.tensor_tensor(ys[0][:, 0, :], faded[0][:], placed[0][:], ALU.add)
-        store(0)
-        scatter(1)
-        nc.gpsimd.tensor_tensor(faded[2][:], olds[2][:], fade_all[:], ALU.mult)
-        scatter(2)
+        ys = [keep.tile([P, PACK, 512], F32, name="y0", tag="w_bf", align_bytes=64), keep.tile([P, PACK, 512], F32, name="y1")]
+        for h, cols in enumerate(halves_u):
+            nc.gpsimd.tensor_tensor(
+                ys[h][:, 0:2, :], olds[h][:, 0:2, :], fade_all[:, cols].unsqueeze(1).to_broadcast([P, 2, 512]), ALU.mult
+            )
+            for t in range(2):
+                nc.gpsimd.tensor_tensor(ys[h][:, t, :], ys[h][:, t, :], placed[t][:, cols], ALU.add)
+                nc.sync.dma_start(out_planes[:, t, cols], ys[h][:, t, :])
+        backs = []
         for h in range(2):
-            cols = slice(h * 512, (h + 1) * 512)
-            nc.vector.tensor_tensor(ys[0][:, 1, cols], faded[1][h][:], placed[1][:, cols], ALU.add)
-        store(1)
-        nc.gpsimd.tensor_tensor(ys[1][:, 0, :], faded[2][:], placed[2][:], ALU.add)
-        store(2)
-        nc.scalar.copy(y_bf[:, :, 0:2], ys[0][:].rearrange("p e u -> p u e"))
-        scatter(3)
+            turned_sb = keep.tile([P, 4, 2, P], F32, name=f"turned_sb{h}")
+            for qq in range(2):
+                turned = bank(qq, [P, 2, 2, P], "turned")
+                for q in range(2):
+                    for e in range(2):
+                        first = (2 * qq + q) * P
+                        nc.tensor.transpose(turned[:, q, e, :], olds[h][:, 2 + e, first:first + P], ident[:])
+                for q in range(2):
+                    b = 4 * h + 2 * qq + q
+                    nc.scalar.activation(turned_sb[:, 2 * qq + q], turned[:, q], ACT.Copy, scale=fade_cols[:, b:b + 1])
+            for e in range(2):
+                back = bank(2 + 2 * h + e, [P, 512], "back")
+                for q in range(4):
+                    nc.tensor.transpose(back[:, q * P:(q + 1) * P], turned_sb[:, q, e, :], ident[:])
+                backs.append(back)
+
+        y_bf = keep.tile([P, U, PACK], BF16, name="y_bf", tag="fade_cols", align_bytes=64)
+        nc.scalar.copy(y_bf[:, 0:512, 0:2], ys[0][:, 0:2, :].rearrange("p t u -> p u t"))
+        for h, cols in enumerate(halves_u):
+            for e in range(2):
+                nc.vector.tensor_tensor(ys[h][:, 2 + e, :], backs[2 * h + e][:], placed[2 + e][:, cols], ALU.add)
+                nc.sync.dma_start(out_planes[:, 2 + e, cols], ys[h][:, 2 + e, :])
+        SPLIT = 128
+        nc.scalar.copy(y_bf[:, 0:512, 2:4], ys[0][:, 2:4, :].rearrange("p t u -> p u t"))
+        nc.scalar.copy(
+            y_bf[:, 512:512 + SPLIT, :].rearrange("p (c i) t -> p c t i", i=4),
+            ys[1][:, :, 0:SPLIT].rearrange("p t (c i) -> p c t i", i=4),
+        )
+        nc.vector.tensor_copy(
+            y_bf[:, 512 + SPLIT:U, :].rearrange("p (c i) t -> p c t i", i=4),
+            ys[1][:, :, SPLIT:512].rearrange("p t (c i) -> p c t i", i=4),
+        )
         y_codes = keep.tile([P, U], U32, name="y_codes", align_bytes=64)
         y_scales = keep.tile([P, U], U8, name="y_scales", align_bytes=64)
         words_out = out_1[0].rearrange("l c r -> l (c r)").bitcast(I32)
-        for h in range(2):
-            cols = slice(h * 512, (h + 1) * 512)
-            nc.vector.tensor_tensor(ys[1][:, 1, cols], faded[3][h][:], placed[3][:, cols], ALU.add)
-        store(3)
-        for h in range(2):
-            cols = slice(h * 512, (h + 1) * 512)
-            nc.vector.tensor_copy(y_bf[:, cols, 2:4], ys[1][:, :, cols].rearrange("p e u -> p u e"))
-        for h in range(2):
-            cols = slice(h * 512, (h + 1) * 512)
+        for cols in halves_u:
             nc.vector.quantize_mx(
                 y_codes[:, cols].bitcast(FP8X4), y_scales[:, cols], y_bf[:, cols, :].rearrange("p u t -> p (u t)")
             )

@@ -18,17 +18,21 @@ ALU = mybir.AluOpType
 AX = mybir.AxisListType
 
 P = 128
-PACK = 4
+PLANES = 4
 PAGE = I // G
-UB = U // P
+STRIPE = 16
+BLOCKS = U // P
+HALF = U // 2
+QUARTER = U // 4
+GPSIMD_WIDTHS = ((HALF, HALF), (HALF, HALF - QUARTER))
 
 
 def tile_attend_summaryrefresh_pl_kernel(tc, hid, wp, bias, old, fade, offs, offs2, out_0, out_1, out_2):
     nc = tc.nc
-    hid_planes = hid.rearrange("(p t) n -> p t n", t=PACK)
-    old_planes = old.rearrange("(p t) u -> p t u", t=PACK)
-    out_planes = out_0.rearrange("(p t) u -> p t u", t=PACK)
-    wp_rows = wp.rearrange("(p j) c -> p j c", j=PACK)
+    hid_planes = hid.rearrange("(p t) n -> p t n", t=PLANES)
+    old_planes = old.rearrange("(p t) u -> p t u", t=PLANES)
+    out_planes = out_0.rearrange("(p t) u -> p t u", t=PLANES)
+    halves_u = [slice(h * HALF, (h + 1) * HALF) for h in range(2)]
 
     with ExitStack() as ctx:
         keep = ctx.enter_context(tc.tile_pool(name="keep", bufs=1))
@@ -37,63 +41,62 @@ def tile_attend_summaryrefresh_pl_kernel(tc, hid, wp, bias, old, fade, offs, off
         def bank(index, shape, name):
             return psum.tile(shape, F32, name=name, tag=f"bank{index}")
 
-        slots = keep.tile([P, I // 16], U16, name="slots")
-        pages = keep.tile([P, G // 16], U16, name="pages")
+        slots = keep.tile([P, I // STRIPE], U16, name="slots")
+        pages = keep.tile([P, G // STRIPE], U16, name="pages")
         fade_rows = keep.tile([P, P], F32, name="fade_rows")
         nc.gpsimd.memset(fade_rows[:], 0.0)
-        pool = []
-        for t in range(PACK):
-            plane = keep.tile([P, T], F32, name=f"pool{t}")
+        tokens = []
+        for t in range(PLANES):
+            plane = keep.tile([P, T], F32, name=f"tokens{t}")
             nc.sync.dma_start(plane[:], hid_planes[:, t, :])
-            pool.append(plane)
+            tokens.append(plane)
             if t == 0:
                 nc.sync.dma_start(slots[:], offs)
-                nc.sync.dma_start(fade_rows[0:UB, :], fade.rearrange("o (b q) -> (o b) q", b=UB))
-        w_raw = keep.tile([P, PACK, D], F32, name="w_raw")
-        nc.sync.dma_start(w_raw[:], wp_rows)
+                nc.sync.dma_start(fade_rows[0:BLOCKS, :], fade.rearrange("o (b q) -> (o b) q", b=BLOCKS))
+        w_raw = keep.tile([P, PLANES, D], F32, name="w_raw")
+        nc.sync.dma_start(w_raw[:], wp.rearrange("(p j) c -> p j c", j=PLANES))
         nc.sync.dma_start(pages[:], offs2)
-        bias4 = keep.tile([P, PACK], F32, name="bias4")
-        nc.sync.dma_start(bias4[:], bias.rearrange("(p t) o -> p (t o)", t=PACK))
-        halves_u = [slice(h * 512, (h + 1) * 512) for h in range(2)]
-        olds = []
+        bias_planes = keep.tile([P, PLANES], F32, name="bias_planes")
+        nc.sync.dma_start(bias_planes[:], bias.rearrange("(p t) o -> p (t o)", t=PLANES))
+        old_halves = []
         for h, cols in enumerate(halves_u):
-            half = keep.tile([P, PACK, 512], F32, name=f"old{h}")
+            half = keep.tile([P, PLANES, HALF], F32, name=f"old{h}")
             nc.sync.dma_start(half[:], old_planes[:, :, cols])
-            olds.append(half)
+            old_halves.append(half)
 
-        warm = keep.tile([P, 2], F32, name="warm")
-        nc.vector.memset(warm[:, 0:1], 0.0)
-        nc.scalar.activation(warm[:, 1:2], warm[:, 0:1], ACT.Tanh)
         ident = keep.tile([P, P], F32, name="ident")
-        make_identity(nc, ident[:])
+        nc.gpsimd.memset(ident[:], 0.0)
+        nc.scalar.activation(ident[:], ident[:], ACT.Tanh)
+        make_identity(nc, ident[:], nomemset=True)
         placed = []
-        for t in range(PACK):
+        for t in range(PLANES):
             window = keep.tile([P, U], F32, name=f"placed{t}")
             (nc.vector if t < 2 else nc.gpsimd).memset(window[:], 0.0)
             placed.append(window)
 
         fade_down = bank(2, [P, P], "fade_down")
         nc.tensor.transpose(fade_down[:], fade_rows[:], ident[:])
-        fade_cols = keep.tile([P, UB], F32, name="fade_cols", tag="fade_cols", align_bytes=64)
-        nc.scalar.copy(fade_cols[:], fade_down[:, 0:UB])
+        fade_cols = keep.tile([P, BLOCKS], F32, name="fade_cols", tag="fade_cols", align_bytes=64)
+        nc.scalar.copy(fade_cols[:], fade_down[:, 0:BLOCKS])
         fade_all = keep.tile([P, U], F32, name="fade_all")
         for h, cols in enumerate(halves_u):
-            spread = bank(3 + h, [P, 512], "spread")
-            for q in range(4):
-                b = 4 * h + q
+            spread = bank(3 + h, [P, HALF], "spread")
+            for q in range(BLOCKS // 2):
+                b = h * BLOCKS // 2 + q
                 nc.tensor.transpose(spread[:, q * P:(q + 1) * P], fade_cols[:, b:b + 1].to_broadcast([P, P]), ident[:])
             nc.scalar.copy(fade_all[:, cols], spread[:])
 
-        hs_bf = keep.tile([P, G, PACK], BF16, name="hs_bf", align_bytes=64)
+        hs_bf = keep.tile([P, G, PLANES], BF16, name="hs_bf", align_bytes=64)
+
         sums_turned = bank(0, [P, 2, 2, P], "sums_turned")
         for t in range(2):
             picked = keep.tile([P, I], F32, name=f"picked{t}")
-            nc.vector.tensor_copy(picked[:], pool[t][:].indirect(slots[:]))
+            nc.vector.tensor_copy(picked[:], tokens[t][:].indirect(slots[:]))
             for gb in range(2):
                 for j in range(PAGE):
                     nc.tensor.matmul(
                         sums_turned[:, t, gb, :],
-                        lhsT=picked[:, gb * 512 + j:(gb + 1) * 512:PAGE],
+                        lhsT=picked[:, gb * P * PAGE + j:(gb + 1) * P * PAGE:PAGE],
                         rhs=ident[:],
                         start=(j == 0),
                         stop=(j == PAGE - 1),
@@ -101,7 +104,7 @@ def tile_attend_summaryrefresh_pl_kernel(tc, hid, wp, bias, old, fade, offs, off
                     )
         pairs_turned = keep.tile([P, 2, P, 2], BF16, name="pairs_turned")
         nc.scalar.activation(pairs_turned[:], sums_turned[:].rearrange("g e b p -> g b p e"), ACT.Copy, scale=1.0 / PAGE)
-        pairs = bank(1, [P, 512], "pairs")
+        pairs = bank(1, [P, HALF], "pairs")
         for gb in range(2):
             nc.tensor.transpose(
                 pairs[:, gb * P:(gb + 1) * P],
@@ -112,100 +115,127 @@ def tile_attend_summaryrefresh_pl_kernel(tc, hid, wp, bias, old, fade, offs, off
         nc.scalar.copy(hs_words[:, 0:2 * G:2], pairs[:, 0:G])
 
         sums = keep.tile([P, 2, G], F32, name="sums")
+        early, late = slice(0, G // 2), slice(G // 2, G)
 
-        def gather(t, first, count):
-            part = keep.tile([P, count, PAGE], F32, name=f"picked{t}_{first}")
-            columns = slice(first * PAGE // 16, (first + count) * PAGE // 16)
-            nc.vector.tensor_copy(part[:].rearrange("p g j -> p (g j)"), pool[t][:].indirect(slots[:, columns]))
+        def gather(t, listed):
+            part = keep.tile([P, G // 2, PAGE], F32, name=f"picked{t}_{listed.start}")
+            columns = slice(listed.start * PAGE // STRIPE, listed.stop * PAGE // STRIPE)
+            nc.vector.tensor_copy(part[:].rearrange("p g j -> p (g j)"), tokens[t][:].indirect(slots[:, columns]))
             return part
 
-        def sum_in_two_steps(part, into):
-            halves = keep.tile([P, part.shape[1], 2], F32, name="halves", tag="halves", bufs=2)
-            nc.gpsimd.tensor_tensor(halves[:], part[:, :, 0:2], part[:, :, 2:4], ALU.add)
-            nc.gpsimd.tensor_tensor(into, halves[:, :, 0], halves[:, :, 1], ALU.add)
+        for t, listed in ((2, early), (2, late), (3, early)):
+            part = gather(t, listed)
+            twos = keep.tile([P, G // 2, 2], F32, name="twos", tag="twos", bufs=2)
+            nc.gpsimd.tensor_tensor(twos[:], part[:, :, 0:2], part[:, :, 2:4], ALU.add)
+            nc.gpsimd.tensor_tensor(sums[:, t - 2, listed], twos[:, :, 0], twos[:, :, 1], ALU.add)
+        nc.gpsimd.tensor_scalar(
+            hs_bf[:, early, 2:4], sums[:, :, early].rearrange("p e g -> p g e"), 1.0 / PAGE, 0.0, ALU.mult, ALU.add
+        )
+        nc.vector.tensor_reduce(sums[:, 1, late], gather(3, late)[:], AX.X, ALU.add)
+        nc.vector.tensor_scalar(hs_bf[:, late, 2:4], sums[:, :, late].rearrange("p e g -> p g e"), 1.0 / PAGE, None, ALU.mult)
 
-        sum_in_two_steps(gather(2, 0, G), sums[:, 0, :])
-        sum_in_two_steps(gather(3, 0, G // 2), sums[:, 1, 0:G // 2])
-        nc.vector.tensor_reduce(sums[:, 1, G // 2:G], gather(3, G // 2, G // 2)[:], AX.X, ALU.add)
-        nc.vector.tensor_scalar(hs_bf[:, :, 2:4], sums[:].rearrange("p e g -> p g e"), 1.0 / PAGE, None, ALU.mult)
+        w_codes, w_scales = [], []
 
-        w_bf = keep.tile([P, PACK, P, PACK], BF16, name="w_bf", tag="w_bf", align_bytes=64)
-        for ts in (slice(0, 2), slice(2, PACK)):
+        def quantise_weights(pair):
+            w_bf = keep.tile([P, 2, P, PLANES], BF16, name=f"w_bf{pair}", tag=f"w_bf{pair}", align_bytes=64)
             nc.scalar.copy(
-                w_bf[:, ts].rearrange("p t m j -> p m j t"),
-                w_raw[:].rearrange("p j (m t) -> p m j t", t=PACK)[:, :, :, ts],
+                w_bf[:].rearrange("p e m j -> p m j e"),
+                w_raw[:].rearrange("p j (m t) -> p m j t", t=PLANES)[:, :, :, 2 * pair:2 * pair + 2],
             )
+            for e in range(2):
+                codes = keep.tile([P, P], U32, name=f"w_codes{2 * pair + e}", align_bytes=64)
+                scales = keep.tile([P, P], U8, name=f"w_scales{2 * pair + e}", align_bytes=64)
+                nc.vector.quantize_mx(codes[:].bitcast(FP8X4), scales[:], w_bf[:, e].rearrange("p m j -> p (m j)"))
+                w_codes.append(codes)
+                w_scales.append(scales)
 
-        hs_codes = keep.tile([P, G], U32, name="hs_codes", align_bytes=64)
+        quantise_weights(0)
+        hs_codes = keep.tile([P, G], U32, name="hs_codes", tag="w_bf0", align_bytes=64)
         hs_scales = keep.tile([P, G], U8, name="hs_scales", align_bytes=64)
         nc.vector.quantize_mx(hs_codes[:].bitcast(FP8X4), hs_scales[:], hs_bf[:].rearrange("p g t -> p (g t)"))
-        zs = []
-        for t in range(PACK):
-            w_codes = keep.tile([P, P], U32, name=f"w_codes{t}", align_bytes=64)
-            w_scales = keep.tile([P, P], U8, name=f"w_scales{t}", align_bytes=64)
-            nc.vector.quantize_mx(w_codes[:].bitcast(FP8X4), w_scales[:], w_bf[:, t].rearrange("p m j -> p (m j)"))
+        quantise_weights(1)
+        z_planes = []
+        for t in range(PLANES):
             z = bank(4 + t, [P, G], f"z{t}")
             nc.tensor.matmul_mx(
-                z[:], lhsT=w_codes[:].bitcast(FP8X4), lhsT_scale=w_scales[:],
+                z[:], lhsT=w_codes[t][:].bitcast(FP8X4), lhsT_scale=w_scales[t][:],
                 rhs=hs_codes[:].bitcast(FP8X4), rhs_scale=hs_scales[:], start=True, stop=True,
             )
-            zs.append(z)
+            z_planes.append(z)
 
-        for t in range(PACK):
-            b = keep.tile([P, G], F32, name=f"fresh{t}")
-            nc.scalar.activation(b[:], zs[t][:], ACT.Tanh, bias=bias4[:, t:t + 1])
-            nc.vector.tensor_copy(placed[t][:].indirect(pages[:]), b[:])
+        for t in range(PLANES):
+            fresh = keep.tile([P, G], F32, name=f"fresh{t}")
+            nc.scalar.activation(fresh[:], z_planes[t][:], ACT.Tanh, bias=bias_planes[:, t:t + 1])
+            nc.vector.tensor_copy(placed[t][:].indirect(pages[:]), fresh[:])
 
-        ys = [keep.tile([P, PACK, 512], F32, name="y0", tag="w_bf", align_bytes=64), keep.tile([P, PACK, 512], F32, name="y1")]
-        for h, cols in enumerate(halves_u):
-            nc.gpsimd.tensor_tensor(
-                ys[h][:, 0:2, :], olds[h][:, 0:2, :], fade_all[:, cols].unsqueeze(1).to_broadcast([P, 2, 512]), ALU.mult
-            )
-            for t in range(2):
-                nc.gpsimd.tensor_tensor(ys[h][:, t, :], ys[h][:, t, :], placed[t][:, cols], ALU.add)
-                nc.sync.dma_start(out_planes[:, t, cols], ys[h][:, t, :])
-        backs = []
+        y_halves = [
+            keep.tile([P, PLANES, HALF], F32, name="y0", tag="w_bf1", align_bytes=64),
+            keep.tile([P, PLANES, HALF], F32, name="y1"),
+        ]
+        for h, widths in enumerate(GPSIMD_WIDTHS):
+            for t, width in enumerate(widths):
+                cols = slice(HALF * h, HALF * h + width)
+                nc.gpsimd.tensor_tensor(y_halves[h][:, t, 0:width], old_halves[h][:, t, 0:width], fade_all[:, cols], ALU.mult)
+            for t, width in enumerate(widths):
+                cols = slice(HALF * h, HALF * h + width)
+                nc.gpsimd.tensor_tensor(y_halves[h][:, t, 0:width], y_halves[h][:, t, 0:width], placed[t][:, cols], ALU.add)
+                nc.sync.dma_start(out_planes[:, t, cols], y_halves[h][:, t, 0:width])
+
+        faded = []
         for h in range(2):
-            turned_sb = keep.tile([P, 4, 2, P], F32, name=f"turned_sb{h}")
-            for qq in range(2):
-                turned = bank(qq, [P, 2, 2, P], "turned")
+            scaled = keep.tile([P, BLOCKS // 2, 2, P], F32, name=f"scaled{h}")
+            for bb in range(2):
+                turned = bank(bb, [P, 2, 2, P], "turned")
                 for q in range(2):
                     for e in range(2):
-                        first = (2 * qq + q) * P
-                        nc.tensor.transpose(turned[:, q, e, :], olds[h][:, 2 + e, first:first + P], ident[:])
+                        first = (2 * bb + q) * P
+                        nc.tensor.transpose(turned[:, q, e, :], old_halves[h][:, 2 + e, first:first + P], ident[:])
                 for q in range(2):
-                    b = 4 * h + 2 * qq + q
-                    nc.scalar.activation(turned_sb[:, 2 * qq + q], turned[:, q], ACT.Copy, scale=fade_cols[:, b:b + 1])
+                    b = h * BLOCKS // 2 + 2 * bb + q
+                    nc.scalar.activation(scaled[:, 2 * bb + q], turned[:, q], ACT.Copy, scale=fade_cols[:, b:b + 1])
             for e in range(2):
-                back = bank(2 + 2 * h + e, [P, 512], "back")
-                for q in range(4):
-                    nc.tensor.transpose(back[:, q * P:(q + 1) * P], turned_sb[:, q, e, :], ident[:])
-                backs.append(back)
+                back = bank(2 + 2 * h + e, [P, HALF], "back")
+                for q in range(BLOCKS // 2):
+                    nc.tensor.transpose(back[:, q * P:(q + 1) * P], scaled[:, q, e, :], ident[:])
+                faded.append(back)
+        rest_scaled = keep.tile([P, 2, P], F32, name="rest_scaled")
+        rest_turned = bank(7, [P, 2, P], "rest_turned")
+        for q in range(2):
+            nc.tensor.transpose(rest_turned[:, q, :], old_halves[1][:, 1, QUARTER + q * P:QUARTER + (q + 1) * P], ident[:])
+        for q in range(2):
+            b = BLOCKS - 2 + q
+            nc.scalar.activation(rest_scaled[:, q], rest_turned[:, q], ACT.Copy, scale=fade_cols[:, b:b + 1])
+        rest_faded = bank(6, [P, QUARTER], "rest_faded")
+        for q in range(2):
+            nc.tensor.transpose(rest_faded[:, q * P:(q + 1) * P], rest_scaled[:, q, :], ident[:])
 
-        y_bf = keep.tile([P, U, PACK], BF16, name="y_bf", tag="fade_cols", align_bytes=64)
-        nc.scalar.copy(y_bf[:, 0:512, 0:2], ys[0][:, 0:2, :].rearrange("p t u -> p u t"))
+        y_bf = keep.tile([P, U, PLANES], BF16, name="y_bf", tag="fade_cols", align_bytes=64)
+        nc.scalar.copy(y_bf[:, 0:HALF, 0:2], y_halves[0][:, 0:2, :].rearrange("p t u -> p u t"))
         for h, cols in enumerate(halves_u):
             for e in range(2):
-                nc.vector.tensor_tensor(ys[h][:, 2 + e, :], backs[2 * h + e][:], placed[2 + e][:, cols], ALU.add)
-                nc.sync.dma_start(out_planes[:, 2 + e, cols], ys[h][:, 2 + e, :])
-        SPLIT = 128
-        nc.scalar.copy(y_bf[:, 0:512, 2:4], ys[0][:, 2:4, :].rearrange("p t u -> p u t"))
-        nc.scalar.copy(
-            y_bf[:, 512:512 + SPLIT, :].rearrange("p (c i) t -> p c t i", i=4),
-            ys[1][:, :, 0:SPLIT].rearrange("p t (c i) -> p c t i", i=4),
-        )
-        nc.vector.tensor_copy(
-            y_bf[:, 512 + SPLIT:U, :].rearrange("p (c i) t -> p c t i", i=4),
-            ys[1][:, :, SPLIT:512].rearrange("p t (c i) -> p c t i", i=4),
-        )
+                nc.vector.tensor_tensor(y_halves[h][:, 2 + e, :], faded[2 * h + e][:], placed[2 + e][:, cols], ALU.add)
+                nc.sync.dma_start(out_planes[:, 2 + e, cols], y_halves[h][:, 2 + e, :])
+        last = slice(U - QUARTER, U)
+        nc.vector.tensor_tensor(y_halves[1][:, 1, QUARTER:HALF], rest_faded[:], placed[1][:, last], ALU.add)
+        nc.sync.dma_start(out_planes[:, 1, last], y_halves[1][:, 1, QUARTER:HALF])
+
         y_codes = keep.tile([P, U], U32, name="y_codes", align_bytes=64)
         y_scales = keep.tile([P, U], U8, name="y_scales", align_bytes=64)
         words_out = out_1[0].rearrange("l c r -> l (c r)").bitcast(I32)
-        for cols in halves_u:
+        nc.scalar.copy(y_bf[:, 0:HALF, 2:4], y_halves[0][:, 2:4, :].rearrange("p t u -> p u t"))
+        for first, copy in ((0, nc.scalar.copy), (QUARTER, nc.vector.tensor_copy)):
+            copy(
+                y_bf[:, HALF + first:HALF + first + QUARTER, :].rearrange("p (c i) t -> p c t i", i=4),
+                y_halves[1][:, :, first:first + QUARTER].rearrange("p t (c i) -> p c t i", i=4),
+            )
+        for cols in (halves_u[0], last, slice(HALF, U - QUARTER)):
             nc.vector.quantize_mx(
                 y_codes[:, cols].bitcast(FP8X4), y_scales[:, cols], y_bf[:, cols, :].rearrange("p u t -> p (u t)")
             )
             nc.sync.dma_start(words_out[:, cols], y_codes[:, cols].bitcast(I32))
-        for q in range(4):
-            engine = nc.sync if q % 2 == 0 else nc.scalar
-            engine.dma_start(out_2[0, 4 * q:4 * q + 4, :].bitcast(I32), y_scales[32 * q:32 * q + 4, :].bitcast(I32))
+        for quadrant in range(4):
+            engine = nc.sync if quadrant % 2 == 0 else nc.scalar
+            engine.dma_start(
+                out_2[0, 4 * quadrant:4 * quadrant + 4, :].bitcast(I32),
+                y_scales[32 * quadrant:32 * quadrant + 4, :].bitcast(I32),
+            )

from contextlib import ExitStack

import concourse.mybir as mybir
from concourse.masks import make_identity

K, T, I, G, U, D = 512, 2048, 1024, 256, 1024, 512
FLOPS = 2 * K * D * G

F32 = mybir.dt.float32
BF16 = mybir.dt.bfloat16
I32 = mybir.dt.int32
U32 = mybir.dt.uint32
U16 = mybir.dt.uint16
U8 = mybir.dt.uint8
FP8X4 = mybir.dt.float8_e4m3fn_x4
ACT = mybir.ActivationFunctionType
ALU = mybir.AluOpType
AX = mybir.AxisListType

P = 128
PLANES = 4
PAGE = I // G
STRIPE = 16
BLOCKS = U // P
HALF = U // 2
QUARTER = U // 4
GPSIMD_WIDTHS = ((HALF, HALF), (HALF, HALF - QUARTER))


def tile_attend_summaryrefresh_pl_kernel(tc, hid, wp, bias, old, fade, offs, offs2, out_0, out_1, out_2):
    nc = tc.nc
    hid_planes = hid.rearrange("(p t) n -> p t n", t=PLANES)
    old_planes = old.rearrange("(p t) u -> p t u", t=PLANES)
    out_planes = out_0.rearrange("(p t) u -> p t u", t=PLANES)
    halves_u = [slice(h * HALF, (h + 1) * HALF) for h in range(2)]

    with ExitStack() as ctx:
        keep = ctx.enter_context(tc.tile_pool(name="keep", bufs=1))
        psum = ctx.enter_context(tc.psum_pool(name="psum", bufs=1))

        def bank(index, shape, name):
            return psum.tile(shape, F32, name=name, tag=f"bank{index}")

        slots = keep.tile([P, I // STRIPE], U16, name="slots")
        pages = keep.tile([P, G // STRIPE], U16, name="pages")
        fade_rows = keep.tile([P, P], F32, name="fade_rows")
        nc.gpsimd.memset(fade_rows[:], 0.0)
        tokens = []
        for t in range(PLANES):
            plane = keep.tile([P, T], F32, name=f"tokens{t}")
            nc.sync.dma_start(plane[:], hid_planes[:, t, :])
            tokens.append(plane)
            if t == 0:
                nc.sync.dma_start(slots[:], offs)
                nc.sync.dma_start(fade_rows[0:BLOCKS, :], fade.rearrange("o (b q) -> (o b) q", b=BLOCKS))
        w_raw = keep.tile([P, PLANES, D], F32, name="w_raw")
        nc.sync.dma_start(w_raw[:], wp.rearrange("(p j) c -> p j c", j=PLANES))
        nc.sync.dma_start(pages[:], offs2)
        bias_planes = keep.tile([P, PLANES], F32, name="bias_planes")
        nc.sync.dma_start(bias_planes[:], bias.rearrange("(p t) o -> p (t o)", t=PLANES))
        old_halves = []
        for h, cols in enumerate(halves_u):
            half = keep.tile([P, PLANES, HALF], F32, name=f"old{h}")
            nc.sync.dma_start(half[:], old_planes[:, :, cols])
            old_halves.append(half)

        ident = keep.tile([P, P], F32, name="ident")
        nc.gpsimd.memset(ident[:], 0.0)
        nc.scalar.activation(ident[:], ident[:], ACT.Tanh)
        make_identity(nc, ident[:], nomemset=True)
        placed = []
        for t in range(PLANES):
            window = keep.tile([P, U], F32, name=f"placed{t}")
            (nc.vector if t < 2 else nc.gpsimd).memset(window[:], 0.0)
            placed.append(window)

        fade_down = bank(2, [P, P], "fade_down")
        nc.tensor.transpose(fade_down[:], fade_rows[:], ident[:])
        fade_cols = keep.tile([P, BLOCKS], F32, name="fade_cols", tag="fade_cols", align_bytes=64)
        nc.scalar.copy(fade_cols[:], fade_down[:, 0:BLOCKS])
        fade_all = keep.tile([P, U], F32, name="fade_all")
        for h, cols in enumerate(halves_u):
            spread = bank(3 + h, [P, HALF], "spread")
            for q in range(BLOCKS // 2):
                b = h * BLOCKS // 2 + q
                nc.tensor.transpose(spread[:, q * P:(q + 1) * P], fade_cols[:, b:b + 1].to_broadcast([P, P]), ident[:])
            nc.scalar.copy(fade_all[:, cols], spread[:])

        hs_bf = keep.tile([P, G, PLANES], BF16, name="hs_bf", align_bytes=64)

        sums_turned = bank(0, [P, 2, 2, P], "sums_turned")
        for t in range(2):
            picked = keep.tile([P, I], F32, name=f"picked{t}")
            nc.vector.tensor_copy(picked[:], tokens[t][:].indirect(slots[:]))
            for gb in range(2):
                for j in range(PAGE):
                    nc.tensor.matmul(
                        sums_turned[:, t, gb, :],
                        lhsT=picked[:, gb * P * PAGE + j:(gb + 1) * P * PAGE:PAGE],
                        rhs=ident[:],
                        start=(j == 0),
                        stop=(j == PAGE - 1),
                        is_transpose=True,
                    )
        pairs_turned = keep.tile([P, 2, P, 2], BF16, name="pairs_turned")
        nc.scalar.activation(pairs_turned[:], sums_turned[:].rearrange("g e b p -> g b p e"), ACT.Copy, scale=1.0 / PAGE)
        pairs = bank(1, [P, HALF], "pairs")
        for gb in range(2):
            nc.tensor.transpose(
                pairs[:, gb * P:(gb + 1) * P],
                pairs_turned[:, gb].rearrange("g p e -> g (p e)").bitcast(F32),
                ident[:],
            )
        hs_words = hs_bf[:].rearrange("p g t -> p (g t)").bitcast(F32)
        nc.scalar.copy(hs_words[:, 0:2 * G:2], pairs[:, 0:G])

        sums = keep.tile([P, 2, G], F32, name="sums")
        early, late = slice(0, G // 2), slice(G // 2, G)

        def gather(t, listed):
            part = keep.tile([P, G // 2, PAGE], F32, name=f"picked{t}_{listed.start}")
            columns = slice(listed.start * PAGE // STRIPE, listed.stop * PAGE // STRIPE)
            nc.vector.tensor_copy(part[:].rearrange("p g j -> p (g j)"), tokens[t][:].indirect(slots[:, columns]))
            return part

        for t, listed in ((2, early), (2, late), (3, early)):
            part = gather(t, listed)
            twos = keep.tile([P, G // 2, 2], F32, name="twos", tag="twos", bufs=2)
            nc.gpsimd.tensor_tensor(twos[:], part[:, :, 0:2], part[:, :, 2:4], ALU.add)
            nc.gpsimd.tensor_tensor(sums[:, t - 2, listed], twos[:, :, 0], twos[:, :, 1], ALU.add)
        nc.gpsimd.tensor_scalar(
            hs_bf[:, early, 2:4], sums[:, :, early].rearrange("p e g -> p g e"), 1.0 / PAGE, 0.0, ALU.mult, ALU.add
        )
        nc.vector.tensor_reduce(sums[:, 1, late], gather(3, late)[:], AX.X, ALU.add)
        nc.vector.tensor_scalar(hs_bf[:, late, 2:4], sums[:, :, late].rearrange("p e g -> p g e"), 1.0 / PAGE, None, ALU.mult)

        w_codes, w_scales = [], []

        def quantise_weights(pair):
            w_bf = keep.tile([P, 2, P, PLANES], BF16, name=f"w_bf{pair}", tag=f"w_bf{pair}", align_bytes=64)
            nc.scalar.copy(
                w_bf[:].rearrange("p e m j -> p m j e"),
                w_raw[:].rearrange("p j (m t) -> p m j t", t=PLANES)[:, :, :, 2 * pair:2 * pair + 2],
            )
            for e in range(2):
                codes = keep.tile([P, P], U32, name=f"w_codes{2 * pair + e}", align_bytes=64)
                scales = keep.tile([P, P], U8, name=f"w_scales{2 * pair + e}", align_bytes=64)
                nc.vector.quantize_mx(codes[:].bitcast(FP8X4), scales[:], w_bf[:, e].rearrange("p m j -> p (m j)"))
                w_codes.append(codes)
                w_scales.append(scales)

        quantise_weights(0)
        hs_codes = keep.tile([P, G], U32, name="hs_codes", tag="w_bf0", align_bytes=64)
        hs_scales = keep.tile([P, G], U8, name="hs_scales", align_bytes=64)
        nc.vector.quantize_mx(hs_codes[:].bitcast(FP8X4), hs_scales[:], hs_bf[:].rearrange("p g t -> p (g t)"))
        quantise_weights(1)
        z_planes = []
        for t in range(PLANES):
            z = bank(4 + t, [P, G], f"z{t}")
            nc.tensor.matmul_mx(
                z[:], lhsT=w_codes[t][:].bitcast(FP8X4), lhsT_scale=w_scales[t][:],
                rhs=hs_codes[:].bitcast(FP8X4), rhs_scale=hs_scales[:], start=True, stop=True,
            )
            z_planes.append(z)

        for t in range(PLANES):
            fresh = keep.tile([P, G], F32, name=f"fresh{t}")
            nc.scalar.activation(fresh[:], z_planes[t][:], ACT.Tanh, bias=bias_planes[:, t:t + 1])
            nc.vector.tensor_copy(placed[t][:].indirect(pages[:]), fresh[:])

        y_halves = [
            keep.tile([P, PLANES, HALF], F32, name="y0", tag="w_bf1", align_bytes=64),
            keep.tile([P, PLANES, HALF], F32, name="y1"),
        ]
        for h, widths in enumerate(GPSIMD_WIDTHS):
            for t, width in enumerate(widths):
                cols = slice(HALF * h, HALF * h + width)
                nc.gpsimd.tensor_tensor(y_halves[h][:, t, 0:width], old_halves[h][:, t, 0:width], fade_all[:, cols], ALU.mult)
            for t, width in enumerate(widths):
                cols = slice(HALF * h, HALF * h + width)
                nc.gpsimd.tensor_tensor(y_halves[h][:, t, 0:width], y_halves[h][:, t, 0:width], placed[t][:, cols], ALU.add)
                nc.sync.dma_start(out_planes[:, t, cols], y_halves[h][:, t, 0:width])

        faded = []
        for h in range(2):
            scaled = keep.tile([P, BLOCKS // 2, 2, P], F32, name=f"scaled{h}")
            for bb in range(2):
                turned = bank(bb, [P, 2, 2, P], "turned")
                for q in range(2):
                    for e in range(2):
                        first = (2 * bb + q) * P
                        nc.tensor.transpose(turned[:, q, e, :], old_halves[h][:, 2 + e, first:first + P], ident[:])
                for q in range(2):
                    b = h * BLOCKS // 2 + 2 * bb + q
                    nc.scalar.activation(scaled[:, 2 * bb + q], turned[:, q], ACT.Copy, scale=fade_cols[:, b:b + 1])
            for e in range(2):
                back = bank(2 + 2 * h + e, [P, HALF], "back")
                for q in range(BLOCKS // 2):
                    nc.tensor.transpose(back[:, q * P:(q + 1) * P], scaled[:, q, e, :], ident[:])
                faded.append(back)
        rest_scaled = keep.tile([P, 2, P], F32, name="rest_scaled")
        rest_turned = bank(7, [P, 2, P], "rest_turned")
        for q in range(2):
            nc.tensor.transpose(rest_turned[:, q, :], old_halves[1][:, 1, QUARTER + q * P:QUARTER + (q + 1) * P], ident[:])
        for q in range(2):
            b = BLOCKS - 2 + q
            nc.scalar.activation(rest_scaled[:, q], rest_turned[:, q], ACT.Copy, scale=fade_cols[:, b:b + 1])
        rest_faded = bank(6, [P, QUARTER], "rest_faded")
        for q in range(2):
            nc.tensor.transpose(rest_faded[:, q * P:(q + 1) * P], rest_scaled[:, q, :], ident[:])

        y_bf = keep.tile([P, U, PLANES], BF16, name="y_bf", tag="fade_cols", align_bytes=64)
        nc.scalar.copy(y_bf[:, 0:HALF, 0:2], y_halves[0][:, 0:2, :].rearrange("p t u -> p u t"))
        for h, cols in enumerate(halves_u):
            for e in range(2):
                nc.vector.tensor_tensor(y_halves[h][:, 2 + e, :], faded[2 * h + e][:], placed[2 + e][:, cols], ALU.add)
                nc.sync.dma_start(out_planes[:, 2 + e, cols], y_halves[h][:, 2 + e, :])
        last = slice(U - QUARTER, U)
        nc.vector.tensor_tensor(y_halves[1][:, 1, QUARTER:HALF], rest_faded[:], placed[1][:, last], ALU.add)
        nc.sync.dma_start(out_planes[:, 1, last], y_halves[1][:, 1, QUARTER:HALF])

        y_codes = keep.tile([P, U], U32, name="y_codes", align_bytes=64)
        y_scales = keep.tile([P, U], U8, name="y_scales", align_bytes=64)
        words_out = out_1[0].rearrange("l c r -> l (c r)").bitcast(I32)
        nc.scalar.copy(y_bf[:, 0:HALF, 2:4], y_halves[0][:, 2:4, :].rearrange("p t u -> p u t"))
        for first, copy in ((0, nc.scalar.copy), (QUARTER, nc.vector.tensor_copy)):
            copy(
                y_bf[:, HALF + first:HALF + first + QUARTER, :].rearrange("p (c i) t -> p c t i", i=4),
                y_halves[1][:, :, first:first + QUARTER].rearrange("p t (c i) -> p c t i", i=4),
            )
        for cols in (halves_u[0], last, slice(HALF, U - QUARTER)):
            nc.vector.quantize_mx(
                y_codes[:, cols].bitcast(FP8X4), y_scales[:, cols], y_bf[:, cols, :].rearrange("p u t -> p (u t)")
            )
            nc.sync.dma_start(words_out[:, cols], y_codes[:, cols].bitcast(I32))
        for quadrant in range(4):
            engine = nc.sync if quadrant % 2 == 0 else nc.scalar
            engine.dma_start(
                out_2[0, 4 * quadrant:4 * quadrant + 4, :].bitcast(I32),
                y_scales[32 * quadrant:32 * quadrant + 4, :].bitcast(I32),
            )
